import numpy as np
import ml_dtypes


def mxq(x, axis, fmt="e4m3"):
    dtype, down = {"e4m3": (ml_dtypes.float8_e4m3fn, 7), "e5m2": (ml_dtypes.float8_e5m2, 14)}[fmt]
    v = np.moveaxis(np.asarray(x, np.float32).astype(ml_dtypes.bfloat16).astype(np.float64), axis, -1)
    blocks = v.reshape(v.shape[:-1] + (-1, 32))
    amax = np.abs(blocks).max(-1, keepdims=True)
    byte = np.maximum(np.where(amax > 0, np.frexp(amax)[1] - 1 + 127, 0) - down, 1)
    scale = np.exp2(byte - 127.0)
    codes = (blocks / scale).astype(np.float32).astype(dtype).astype(np.float64)
    return np.moveaxis((codes * scale).reshape(v.shape), -1, axis)


WIDE = False


def mx_kscale(k):
    if not WIDE:
        return np.ones(k)
    levels = np.array([10, -10, 5, -5, 0])
    if k % 512:
        return np.exp2(np.random.permutation(np.resize(levels, k // 32))).repeat(32)
    a = np.empty((k // 512, 16))
    for p in range(k // 512):
        a[p, :8] = np.random.permutation(np.resize(levels, 8))
        for g in range(8):
            far = levels[np.abs(levels - a[p, g]) >= 10]
            a[p, g + 8] = far[np.random.randint(len(far))]
    return np.exp2(a.ravel()).repeat(32)


def f64(x):
    return np.asarray(x).astype(np.float64)


def striped(idx):
    return np.tile(np.asarray(idx).reshape(-1, 16).T, (8, 1)).astype(np.uint16)


def unstriped(offs):
    return offs[:16].T.reshape(-1).astype(np.int64)


E2M1 = np.array([0.0, 0.5, 1.0, 1.5, 2.0, 3.0, 4.0, 6.0, -0.0, -0.5, -1.0, -1.5, -2.0, -3.0, -4.0, -6.0])


def pack_weight(w, fmt):
    k, n = w.shape
    w = f64(np.asarray(w, np.float32).astype(ml_dtypes.bfloat16)).reshape(k // 32, 32, n)
    amax = np.abs(w).max(1)
    if fmt == "e4m3":
        byte = np.frexp(amax)[1] - 1 + 127 - 7
    else:
        mant, ex = np.frexp(amax / 6.0)
        byte = np.where(mant > 0.5, ex, ex - 1) + 127
    byte = np.clip(np.where(amax > 0, byte, 1), 1, 254)
    scaled = (w * np.exp2(127.0 - byte)[:, None, :]).reshape(k, n).astype(np.float32)
    by_word = np.ascontiguousarray(scaled.reshape(k // 512, 128, 4, n).transpose(0, 1, 3, 2))
    if fmt == "e4m3":
        words = by_word.astype(ml_dtypes.float8_e4m3fn).view(np.uint8)
    else:
        c = by_word.astype(ml_dtypes.float4_e2m1fn).view(np.uint8) & 0xF
        words = (c[..., 0::2] | (c[..., 1::2] << 4)).reshape(k // 512, 128, 2 * n)
    return np.ascontiguousarray(words), np.ascontiguousarray(byte.astype(np.uint8).reshape(k // 512, 16, n))


def unpack_weight(words, scales, fmt):
    g, _, n = scales.shape
    words = np.ascontiguousarray(words).reshape(g, 128, n, -1)
    if fmt == "e4m3":
        vals = words.view(ml_dtypes.float8_e4m3fn).astype(np.float64)
    else:
        nib = np.empty((g, 128, n, 4), np.uint8)
        nib[..., 0::2] = words & 0xF
        nib[..., 1::2] = words >> 4
        vals = E2M1[nib]
    vals = vals * np.repeat(np.exp2(scales.astype(np.float64) - 127.0), 8, axis=1)[..., None]
    return vals.transpose(0, 1, 3, 2).reshape(g * 512, n)


def bf(x):
    return np.asarray(x, np.float32).astype(ml_dtypes.bfloat16)


def planes(Y):
    r, m = Y.shape
    b = f64(bf(Y)).reshape(r // 32, 32, m)
    amax = np.abs(b).max(1)
    byte = np.clip(np.where(amax > 0, np.frexp(amax)[1] - 1 + 127 - 7, 1), 1, 254)
    codes = (b * np.exp2(127.0 - byte)[:, None, :]).reshape(r, m).astype(np.float32).astype(ml_dtypes.float8_e4m3fn).view(np.uint8)
    words = codes.reshape(r // 512, 128, 4, m).transpose(0, 1, 3, 2)
    return np.ascontiguousarray(words), np.ascontiguousarray(byte.astype(np.uint8).reshape(r // 512, 16, m))


D, E, T, I, Q = 512, 512, 2048, 512, 256


def setup_inputs():
    n = np.random.standard_normal
    idx = np.random.permutation(T)[:I]
    fd = mx_kscale(D)
    fi = mx_kscale(I)
    ti = np.ones(T)
    ti[idx] = fi
    keysp = pack_weight(n((D, T)) / fd[:, None], "e2m1")
    return {
        "query": (n((D, Q)) * 0.7 / np.sqrt(D) * fd[:, None]).astype(np.float32),
        "dquery": (n((D, Q)) * 1.0 / np.sqrt(D) * fd[:, None]).astype(np.float32),
        "query2": (n((D, Q)) * 0.7 / np.sqrt(D) * fd[:, None]).astype(np.float32),
        "dquery2": (n((D, Q)) * 1.0 / np.sqrt(D) * fd[:, None]).astype(np.float32),
        "keys_words": keysp[0],
        "keys_scales": keysp[1],
        "os": (np.random.uniform(8.0, 32.0, (1, I)) * fi).astype(np.float32),
        "vals": (n((E, T)) / ti).astype(np.float32),
        "offs": striped(idx),
    }


def reference(query, dquery, query2, dquery2, keys_words, keys_scales, os, vals, offs):
    idx = unstriped(offs)
    keysu = unpack_weight(keys_words, keys_scales, "e2m1")
    queryq = mxq(f64(query), 0, "e4m3")
    keysidxg = keysu[:, idx]
    a = queryq.T @ keysidxg
    dqueryq = mxq(f64(dquery), 0, "e4m3")
    ta = dqueryq.T @ keysidxg
    query2q = mxq(f64(query2), 0, "e4m3")
    b = query2q.T @ keysidxg
    dquery2q = mxq(f64(dquery2), 0, "e4m3")
    tb = dquery2q.T @ keysidxg
    pa = np.exp(a - np.max(a, axis=1, keepdims=True))
    wa = pa / np.sum(pa, axis=1, keepdims=True)
    pb = np.exp(b - np.max(b, axis=1, keepdims=True))
    wb = pb / np.sum(pb, axis=1, keepdims=True)
    tpa = ta * pa
    twa = (tpa - np.sum(tpa, axis=1, keepdims=True) * pa / np.sum(pa, axis=1, keepdims=True)) / np.sum(pa, axis=1, keepdims=True)
    tpb = tb * pb
    twb = (tpb - np.sum(tpb, axis=1, keepdims=True) * pb / np.sum(pb, axis=1, keepdims=True)) / np.sum(pb, axis=1, keepdims=True)
    tw = (twa * wb + twb * wa - (twa + twb) * wa * wb / (wa + wb)) / (wa + wb)
    wo1 = tw * f64(os)
    wt1 = wo1.T
    vt1 = f64(vals)[:, idx].T
    vt1q = mxq(vt1, 0, "e4m3")
    wt1q = mxq(wt1, 0, "e4m3")
    o = vt1q.T @ wt1q
    words, scales = planes(o)
    return o, words, scales

@@ -1,0 +1,269 @@
+from contextlib import ExitStack
+
+import concourse.mybir as mybir
+from concourse.masks import make_identity
+
+D, E, T, I, Q = 512, 512, 2048, 512, 256
+FLOPS = 2 * (4 * D * Q * I + I * E * Q)
+
+F32 = mybir.dt.float32
+BF16 = mybir.dt.bfloat16
+I32 = mybir.dt.int32
+U32 = mybir.dt.uint32
+U16 = mybir.dt.uint16
+U8 = mybir.dt.uint8
+FP8X4 = mybir.dt.float8_e4m3fn_x4
+FP4X4 = mybir.dt.float4_e2m1fn_x4
+ALU = mybir.AluOpType
+ACT = mybir.ActivationFunctionType
+
+P = 128
+PACK = 4
+QT = Q // P
+
+
+def tile_attend_ttagreement_pl_kernel(tc, query, dquery, query2, dquery2, keys_words, keys_scales, slot_factor, vals, offs,
+                                       out_0, out_1, out_2):
+    nc = tc.nc
+    with ExitStack() as ctx:
+        sb = ctx.enter_context(tc.tile_pool(name="sb", bufs=1))
+        ps = ctx.enter_context(tc.psum_pool(name="ps", bufs=1))
+
+        def tile(shape, dtype, name, slot=None):
+            return sb.tile(shape, dtype, name=name, tag=slot or name, align_bytes=64)
+
+        def bank(n, name):
+            return ps.tile([P, 512], F32, name=name, tag="bank%d" % n)
+
+        offsets = tile([P, I // 16], U16, name="offsets")
+        nc.sync.dma_start(offsets[:], offs)
+        kscale = tile([P, T], U8, name="kscale")
+        nc.gpsimd.memset(kscale[:].bitcast(I32), 0)
+        kword = tile([P, T], U16, name="kword")
+        nc.sync.dma_start(kword[:].bitcast(I32), keys_words[0].bitcast(I32))
+        for g in range(4):
+            nc.scalar.dma_start(kscale[32 * g:32 * g + 4, :].bitcast(I32),
+                                keys_scales[0, 4 * g:4 * g + 4, :].bitcast(I32))
+        qnames = ("qa", "qb", "da", "db")
+        qsrc = dict(zip(qnames, (query, query2, dquery, dquery2)))
+        qraw = {}
+
+        def load_query(n):
+            qraw[n] = tile([P, PACK, Q], F32, name="raw_" + n, slot="kword" if n == "db" else None)
+            nc.sync.dma_start(qraw[n][:], qsrc[n].rearrange("(p j) q -> p j q", j=PACK))
+
+        for n in qnames[:3]:
+            load_query(n)
+        vraw = []
+        vals_dealt = vals.rearrange("(p j) t -> j p t", j=PACK)
+
+        def load_values(j, slot):
+            vraw.append(tile([P, T], F32, name="vraw%d" % j, slot=slot))
+            nc.sync.dma_start(vraw[j][:], vals_dealt[j])
+
+        ident = tile([P, P], F32, name="ident")
+        make_identity(nc, ident[:])
+
+        ks_g = tile([P, I], U8, name="ks_g")
+        kw_g = tile([P, I], U16, name="kw_g")
+        ks_d = tile([P, I], U8, name="ks_d")
+        kw_d = tile([P, I], U16, name="kw_d")
+        nc.vector.tensor_copy(kw_g[:], kword[:].indirect(offsets[:]))
+        nc.vector.tensor_copy(ks_g[:], kscale[:].indirect(offsets[:]))
+        nc.vector.tensor_copy(kw_d[:].rearrange("p (t s) -> p s t", t=PACK), kw_g[:].rearrange("p (s t) -> p s t", t=PACK))
+        nc.vector.tensor_copy(ks_d[:].rearrange("p (t s) -> p s t", t=PACK), ks_g[:].rearrange("p (s t) -> p s t", t=PACK))
+
+        load_query("db")
+        load_values(0, "ks_g")
+        os_col = tile([P, PACK], F32, name="os_col", slot="kw_g")
+        nc.sync.dma_start(os_col[:], slot_factor.rearrange("o (s t) -> (o s) t", t=PACK))
+
+        qcode, qscale = {}, {}
+
+        def regroup(n):
+            grouped = tile([P, Q, PACK], BF16, name="grp_" + n)
+            dst = grouped[:].rearrange("p (c i) t -> p c t i", i=4)
+            src = qraw[n][:].rearrange("p t (c i) -> p c t i", i=4)
+            nc.scalar.activation(dst, src, ACT.Copy)
+            return grouped
+
+        def quantise_q(n, grouped):
+            qcode[n] = tile([P, Q], U32, name="code_" + n, slot="kscale" if n == "qa" else None)
+            qscale[n] = tile([P, Q], U8, name="scale_" + n)
+            nc.vector.quantize_mx(out=qcode[n][:].bitcast(FP8X4), scales=qscale[n][:],
+                                  in_=grouped[:].rearrange("p q t -> p (q t)"))
+
+        def score(out, n, k, start=True):
+            cols = slice(k * P, (k + 1) * P)
+            nc.tensor.matmul_mx(out=out[:], lhsT=qcode[n][:, cols].bitcast(FP8X4), lhsT_scale=qscale[n][:, cols],
+                                rhs=kw_d[:].bitcast(FP4X4), rhs_scale=ks_d[:], start=start, stop=True)
+
+        negmax = tile([P, 4], F32, name="negmax")
+        rowsum = tile([P, 4], F32, name="rowsum")
+        tsum = tile([P, 4], F32, name="tsum")
+        junk = [tile([P, I], F32, name="junk%d" % k) for k in range(2 * QT)]
+
+        quantise_q("qa", regroup("qa"))
+        load_values(1, "raw_qa")
+        sa = [bank(k, "sa%d" % k) for k in range(QT)]
+        for k in range(QT):
+            score(sa[k], "qa", k)
+        quantise_q("qb", regroup("qb"))
+        load_values(2, "raw_qb")
+        sb_neg = [bank(2 + k, "sbn%d" % k) for k in range(QT)]
+        for k in range(QT):
+            score(sb_neg[k], "qb", k)
+        g_da = regroup("da")
+        load_values(3, "raw_da")
+        quantise_q("da", g_da)
+        ta = [bank(4 + k, "ta%d" % k) for k in range(QT)]
+        for k in range(QT):
+            score(ta[k], "da", k)
+        g_db = regroup("db")
+        nega = [tile([P, I], F32, name="nega%d" % k) for k in range(QT)]
+        negb = [tile([P, I], F32, name="negb%d" % k) for k in range(QT)]
+        wa = [tile([P, I], F32, name="wa%d" % k) for k in range(QT)]
+        gap = [tile([P, I], F32, name="gap%d" % k) for k in range(QT)]
+        pa = [tile([P, I], F32, name="pa%d" % k) for k in range(QT)]
+        pb = [tile([P, I], F32, name="pb%d" % k) for k in range(QT)]
+        for k in range(QT):
+            nc.vector.tensor_scalar(nega[k][:], sa[k][:], -1.0, None, ALU.mult, ALU.min, accum_out=negmax[:, k:k + 1])
+            nc.scalar.activation(pa[k][:], sa[k][:], ACT.Exp, bias=negmax[:, k:k + 1], scale=1.0,
+                                 accum_out=rowsum[:, k:k + 1])
+        quantise_q("db", g_db)
+        tb = [bank(6 + k, "tb%d" % k) for k in range(QT)]
+        for k in range(QT):
+            score(tb[k], "db", k)
+        for k in range(QT):
+            nc.vector.tensor_scalar(negb[k][:], sb_neg[k][:], -1.0, None, ALU.mult, ALU.min,
+                                    accum_out=negmax[:, 3 - k:4 - k])
+            nc.scalar.activation(pb[k][:], sb_neg[k][:], ACT.Exp, bias=negmax[:, 3 - k:4 - k], scale=1.0,
+                                 accum_out=rowsum[:, 3 - k:4 - k])
+        for k in range(QT):
+            nc.gpsimd.tensor_tensor(gap[k][:], nega[k][:], negb[k][:], ALU.subtract)
+        logsum = tile([P, 4], F32, name="logsum")
+        nc.scalar.activation(logsum[:], rowsum[:], ACT.Ln)
+
+
+        for k in range(QT):
+            nc.vector.scalar_tensor_tensor(junk[k][:], ta[k][:], 1.0, pa[k][:], ALU.mult, ALU.mult,
+                                           accum_out=tsum[:, k:k + 1])
+        inv = tile([P, 4], F32, name="inv")
+        nc.vector.reciprocal(inv[:], rowsum[:])
+        for k in range(QT):
+            nc.gpsimd.tensor_scalar(wa[k][:], pa[k][:], inv[:, k:k + 1], 0.0, ALU.mult, ALU.add)
+        lse = tile([P, 4], F32, name="lse")
+        nc.vector.tensor_tensor(lse[:], logsum[:], negmax[:], ALU.subtract)
+        shift = tile([P, 4], F32, name="shift")
+        nc.vector.tensor_tensor(shift[:], lse[:, ::-1], lse[:], ALU.subtract)
+        for k in range(QT):
+            nc.vector.scalar_tensor_tensor(junk[2 + k][:], tb[k][:], 1.0, pb[k][:], ALU.mult, ALU.mult,
+                                           accum_out=tsum[:, 3 - k:4 - k])
+        mean = tile([P, 4], F32, name="mean")
+        nc.vector.tensor_tensor(mean[:], tsum[:], inv[:], ALU.mult)
+
+        vgrp = tile([P, PACK, P, PACK], BF16, name="vgrp", slot="gap1")
+        vcode = tile([P, E], U32, name="vcode")
+        vscale = tile([P, E], U8, name="vscale")
+        vbank, vpair = {}, {}
+
+        def values(j):
+            if j % 2 == 0:
+                vpair[j // 2] = tile([P, 2, I], BF16, name="vg%d" % j, slot=("lse", "r0")[j // 2])
+            vg = vpair[j // 2][:, j % 2, :]
+            nc.vector.tensor_copy(vg, vraw[j][:].indirect(offsets[:]))
+            if j % 2 == 0:
+                vbank[j // 2] = bank(2 + j // 2, "vbank%d" % (j // 2))
+            vb = vbank[j // 2][:].rearrange("p (j u m) -> p j u m", j=2, u=2)
+            words = vg.bitcast(F32)
+            for u in range(2):
+                nc.tensor.transpose(vb[:, j % 2, u, :], words[:, u:I // 2:2], ident[:])
+            nc.scalar.copy(vgrp[:, j].rearrange("p m t -> p (m t)").bitcast(F32).rearrange("p (m u) -> p m u", u=2),
+                           vb[:, j % 2].rearrange("p u m -> p m u"))
+
+        def quantise_v(j0, j1):
+            nc.vector.quantize_mx(out=vcode[:, j0 * P:j1 * P].bitcast(FP8X4), scales=vscale[:, j0 * P:j1 * P],
+                                  in_=vgrp[:, j0:j1].rearrange("p j m t -> p (j m t)"))
+
+        r = [tile([P, I], F32, name="r%d" % k) for k in range(QT)]
+        rbar = [tile([P, I], F32, name="rbar%d" % k) for k in range(QT)]
+        for k in range(QT):
+            nc.scalar.activation(rbar[k][:], gap[k][:], ACT.Sigmoid, bias=shift[:, 3 - k:4 - k], scale=1.0)
+            nc.scalar.activation(r[k][:], gap[k][:], ACT.Sigmoid, bias=shift[:, k:k + 1], scale=-1.0)
+
+        values(0)
+        values(1)
+        wgrp = tile([P, Q, PACK], BF16, name="wgrp")
+        wcode = tile([P, Q], U32, name="wcode")
+        wscale = tile([P, Q], U8, name="wscale")
+        hs, at = [], []
+
+        def terms(k):
+            h = tile([P, I], F32, name="h%d" % k)
+            a1 = tile([P, I], F32, name="a1_%d" % k)
+            a2 = tile([P, I], F32, name="a2_%d" % k)
+            nc.gpsimd.tensor_tensor(h[:], rbar[k][:], wa[k][:], ALU.mult)
+            ht = bank(k, "ht%d" % k)
+            hs.append(tile([P, PACK, P], F32, name="hs%d" % k))
+            for t in range(PACK):
+                nc.tensor.transpose(ht[:, t * P:(t + 1) * P], h[:, t * P:(t + 1) * P], ident[:])
+            for t in range(PACK):
+                nc.scalar.activation(hs[k][:, t, :], ht[:, t * P:(t + 1) * P], ACT.Copy, scale=os_col[:, t:t + 1])
+            nc.vector.scalar_tensor_tensor(a1[:], ta[k][:], mean[:, k:k + 1], rbar[k][:], ALU.subtract, ALU.mult)
+            nc.vector.scalar_tensor_tensor(a2[:], tb[k][:], mean[:, 3 - k:4 - k], r[k][:], ALU.subtract, ALU.mult)
+            at.append(bank(4 + k, "at%d" % k))
+            for t in range(PACK):
+                cols = slice(t * P, (t + 1) * P)
+                nc.tensor.matmul(at[k][:, cols], a1[:, cols], ident[:], start=True, stop=False, is_transpose=True)
+                nc.tensor.matmul(at[k][:, cols], a2[:, cols], ident[:], start=False, stop=True, is_transpose=True)
+
+        def weigh(k):
+            nc.vector.tensor_tensor(wgrp[:, k * P:(k + 1) * P, :], at[k][:].rearrange("p (t q) -> p q t", t=PACK),
+                                    hs[k][:].rearrange("p t q -> p q t"), ALU.mult)
+
+        def quantise_w(k):
+            cols = slice(k * P, (k + 1) * P)
+            nc.vector.quantize_mx(out=wcode[:, cols].bitcast(FP8X4), scales=wscale[:, cols],
+                                  in_=wgrp[:, cols, :].rearrange("p q t -> p (q t)"))
+
+        osb = tile([P, PACK, Q], F32, name="osb")
+        ogrp = tile([P, Q, PACK], BF16, name="ogrp")
+        ocode = tile([P, Q], U32, name="ocode")
+        oscale = tile([P, Q], U8, name="oscale")
+        out_rows = out_0.rearrange("(p j) q -> p j q", j=PACK)
+
+        def product(k):
+            cols = slice(k * P, (k + 1) * P)
+            ob = bank(6 + k, "ob%d" % k)
+            for j in range(PACK):
+                ecols = slice(j * P, (j + 1) * P)
+                nc.tensor.matmul_mx(out=ob[:, ecols], lhsT=vcode[:, ecols].bitcast(FP8X4), lhsT_scale=vscale[:, ecols],
+                                    rhs=wcode[:, cols].bitcast(FP8X4), rhs_scale=wscale[:, cols], start=True, stop=True)
+            regroup_out = nc.scalar.copy if k == 0 else nc.vector.tensor_copy
+            regroup_out(ogrp[:, cols, :], ob[:].rearrange("p (j q) -> p q j", j=PACK))
+            nc.scalar.copy(osb[:, :, cols], ob[:].rearrange("p (j q) -> p j q", j=PACK))
+            nc.sync.dma_start(out_rows[:, :, cols], osb[:, :, cols])
+
+        def quantise_out(k):
+            cols = slice(k * P, (k + 1) * P)
+            nc.vector.quantize_mx(out=ocode[:, cols].bitcast(FP8X4), scales=oscale[:, cols],
+                                  in_=ogrp[:, cols, :].rearrange("p q t -> p (q t)"))
+
+        terms(0)
+        quantise_v(0, 2)
+        values(2)
+        values(3)
+        terms(1)
+        weigh(0)
+        quantise_v(2, 4)
+        quantise_w(0)
+        product(0)
+        weigh(1)
+        quantise_w(1)
+        quantise_out(0)
+        product(1)
+        quantise_out(1)
+        nc.sync.dma_start(out_1[0].rearrange("p c r -> p (c r)").bitcast(I32), ocode[:].bitcast(I32))
+        for g in range(4):
+            queue = nc.scalar if g % 2 else nc.sync
+            queue.dma_start(out_2[0, 4 * g:4 * g + 4, :].bitcast(I32), oscale[32 * g:32 * g + 4, :].bitcast(I32))

@@ -15,6 +15,7 @@ U8 = mybir.dt.uint8
 FP8X4 = mybir.dt.float8_e4m3fn_x4
 FP4X4 = mybir.dt.float4_e2m1fn_x4
 ALU = mybir.AluOpType
+AX = mybir.AxisListType
 ACT = mybir.ActivationFunctionType
 
 P = 128
@@ -70,8 +71,8 @@ def tile_attend_ttagreement_pl_kernel(tc, query, dquery, query2, dquery2, keys_w
         kw_d = tile([P, I], U16, name="kw_d")
         nc.vector.tensor_copy(kw_g[:], kword[:].indirect(offsets[:]))
         nc.vector.tensor_copy(ks_g[:], kscale[:].indirect(offsets[:]))
-        nc.vector.tensor_copy(kw_d[:].rearrange("p (t s) -> p s t", t=PACK), kw_g[:].rearrange("p (s t) -> p s t", t=PACK))
-        nc.vector.tensor_copy(ks_d[:].rearrange("p (t s) -> p s t", t=PACK), ks_g[:].rearrange("p (s t) -> p s t", t=PACK))
+        nc.vector.tensor_copy(kw_d[:].rearrange("p (t s) -> p t s", t=PACK), kw_g[:].rearrange("p (s t) -> p t s", t=PACK))
+        nc.vector.tensor_copy(ks_d[:].rearrange("p (t s) -> p t s", t=PACK), ks_g[:].rearrange("p (s t) -> p t s", t=PACK))
 
         load_query("db")
         load_values(0, "ks_g")
@@ -84,7 +85,7 @@ def tile_attend_ttagreement_pl_kernel(tc, query, dquery, query2, dquery2, keys_w
             grouped = tile([P, Q, PACK], BF16, name="grp_" + n)
             dst = grouped[:].rearrange("p (c i) t -> p c t i", i=4)
             src = qraw[n][:].rearrange("p t (c i) -> p c t i", i=4)
-            nc.scalar.activation(dst, src, ACT.Copy)
+            nc.scalar.activation(dst, src, ACT.Copy, scale=-1.0 if n == "qb" else 1.0)
             return grouped
 
         def quantise_q(n, grouped):
@@ -93,10 +94,10 @@ def tile_attend_ttagreement_pl_kernel(tc, query, dquery, query2, dquery2, keys_w
             nc.vector.quantize_mx(out=qcode[n][:].bitcast(FP8X4), scales=qscale[n][:],
                                   in_=grouped[:].rearrange("p q t -> p (q t)"))
 
-        def score(out, n, k, start=True):
+        def score(out, n, k, start=True, stop=True):
             cols = slice(k * P, (k + 1) * P)
             nc.tensor.matmul_mx(out=out[:], lhsT=qcode[n][:, cols].bitcast(FP8X4), lhsT_scale=qscale[n][:, cols],
-                                rhs=kw_d[:].bitcast(FP4X4), rhs_scale=ks_d[:], start=start, stop=True)
+                                rhs=kw_d[:].bitcast(FP4X4), rhs_scale=ks_d[:], start=start, stop=stop)
 
         negmax = tile([P, 4], F32, name="negmax")
         rowsum = tile([P, 4], F32, name="rowsum")
@@ -115,32 +116,33 @@ def tile_attend_ttagreement_pl_kernel(tc, query, dquery, query2, dquery2, keys_w
             score(sb_neg[k], "qb", k)
         g_da = regroup("da")
         load_values(3, "raw_da")
+        g_db = regroup("db")
+        nega = tile([P, I], F32, name="nega")
+        pa = [tile([P, I], F32, name="pa%d" % k) for k in range(QT)]
+        pb = [tile([P, I], F32, name="pb%d" % k) for k in range(QT)]
+        for k in range(QT):
+            if k == 0:
+                nc.vector.tensor_scalar(nega[:], sa[k][:], -1.0, None, ALU.mult, ALU.min, accum_out=negmax[:, k:k + 1])
+            else:
+                nc.vector.tensor_reduce(negmax[:, k:k + 1], sa[k][:], AX.X, ALU.max, negate=True)
+            nc.scalar.activation(pa[k][:], sa[k][:], ACT.Exp, bias=negmax[:, k:k + 1], scale=1.0,
+                                 accum_out=rowsum[:, k:k + 1])
+        for k in range(QT):
+            nc.vector.tensor_reduce(negmax[:, 3 - k:4 - k], sb_neg[k][:], AX.X, ALU.min)
+            nc.scalar.activation(pb[k][:], sb_neg[k][:], ACT.Exp, bias=negmax[:, 3 - k:4 - k], scale=-1.0,
+                                 accum_out=rowsum[:, 3 - k:4 - k])
         quantise_q("da", g_da)
         ta = [bank(4 + k, "ta%d" % k) for k in range(QT)]
         for k in range(QT):
             score(ta[k], "da", k)
-        g_db = regroup("db")
-        nega = [tile([P, I], F32, name="nega%d" % k) for k in range(QT)]
-        negb = [tile([P, I], F32, name="negb%d" % k) for k in range(QT)]
-        wa = [tile([P, I], F32, name="wa%d" % k) for k in range(QT)]
-        gap = [tile([P, I], F32, name="gap%d" % k) for k in range(QT)]
-        pa = [tile([P, I], F32, name="pa%d" % k) for k in range(QT)]
-        pb = [tile([P, I], F32, name="pb%d" % k) for k in range(QT)]
-        for k in range(QT):
-            nc.vector.tensor_scalar(nega[k][:], sa[k][:], -1.0, None, ALU.mult, ALU.min, accum_out=negmax[:, k:k + 1])
-            nc.scalar.activation(pa[k][:], sa[k][:], ACT.Exp, bias=negmax[:, k:k + 1], scale=1.0,
-                                 accum_out=rowsum[:, k:k + 1])
         quantise_q("db", g_db)
         tb = [bank(6 + k, "tb%d" % k) for k in range(QT)]
         for k in range(QT):
             score(tb[k], "db", k)
-        for k in range(QT):
-            nc.vector.tensor_scalar(negb[k][:], sb_neg[k][:], -1.0, None, ALU.mult, ALU.min,
-                                    accum_out=negmax[:, 3 - k:4 - k])
-            nc.scalar.activation(pb[k][:], sb_neg[k][:], ACT.Exp, bias=negmax[:, 3 - k:4 - k], scale=1.0,
-                                 accum_out=rowsum[:, 3 - k:4 - k])
-        for k in range(QT):
-            nc.gpsimd.tensor_tensor(gap[k][:], nega[k][:], negb[k][:], ALU.subtract)
+        gap = [tile([P, I], F32, name="gap0"), bank(0, "gap1")]
+        nc.vector.tensor_tensor(gap[0][:], sb_neg[0][:], nega[:], ALU.subtract)
+        score(gap[1], "qa", 1, stop=False)
+        score(gap[1], "qb", 1, start=False)
         logsum = tile([P, 4], F32, name="logsum")
         nc.scalar.activation(logsum[:], rowsum[:], ACT.Ln)
 
@@ -150,8 +152,6 @@ def tile_attend_ttagreement_pl_kernel(tc, query, dquery, query2, dquery2, keys_w
                                            accum_out=tsum[:, k:k + 1])
         inv = tile([P, 4], F32, name="inv")
         nc.vector.reciprocal(inv[:], rowsum[:])
-        for k in range(QT):
-            nc.gpsimd.tensor_scalar(wa[k][:], pa[k][:], inv[:, k:k + 1], 0.0, ALU.mult, ALU.add)
         lse = tile([P, 4], F32, name="lse")
         nc.vector.tensor_tensor(lse[:], logsum[:], negmax[:], ALU.subtract)
         shift = tile([P, 4], F32, name="shift")
@@ -162,24 +162,25 @@ def tile_attend_ttagreement_pl_kernel(tc, query, dquery, query2, dquery2, keys_w
         mean = tile([P, 4], F32, name="mean")
         nc.vector.tensor_tensor(mean[:], tsum[:], inv[:], ALU.mult)
 
-        vgrp = tile([P, PACK, P, PACK], BF16, name="vgrp", slot="gap1")
+        vgrp = tile([P, PACK, P, PACK], BF16, name="vgrp", slot="shift")
         vcode = tile([P, E], U32, name="vcode")
         vscale = tile([P, E], U8, name="vscale")
-        vbank, vpair = {}, {}
+        vg, vpair = {}, {}
 
-        def values(j):
+        def gather_values(j):
             if j % 2 == 0:
                 vpair[j // 2] = tile([P, 2, I], BF16, name="vg%d" % j, slot=("lse", "r0")[j // 2])
-            vg = vpair[j // 2][:, j % 2, :]
-            nc.vector.tensor_copy(vg, vraw[j][:].indirect(offsets[:]))
-            if j % 2 == 0:
-                vbank[j // 2] = bank(2 + j // 2, "vbank%d" % (j // 2))
-            vb = vbank[j // 2][:].rearrange("p (j u m) -> p j u m", j=2, u=2)
-            words = vg.bitcast(F32)
-            for u in range(2):
-                nc.tensor.transpose(vb[:, j % 2, u, :], words[:, u:I // 2:2], ident[:])
-            nc.scalar.copy(vgrp[:, j].rearrange("p m t -> p (m t)").bitcast(F32).rearrange("p (m u) -> p m u", u=2),
-                           vb[:, j % 2].rearrange("p u m -> p m u"))
+            vg[j] = vpair[j // 2][:, j % 2, :]
+            nc.vector.tensor_copy(vg[j], vraw[j][:].indirect(offsets[:]))
+
+        def turn_values(pair):
+            vb = bank(2 + pair, "vbank%d" % pair)[:].rearrange("p (j u m) -> p j u m", j=2, u=2)
+            for j in range(2):
+                words = vg[2 * pair + j].bitcast(F32)
+                for u in range(2):
+                    nc.tensor.transpose(vb[:, j, u, :], words[:, u:I // 2:2], ident[:])
+            dst = vgrp[:, 2 * pair:2 * pair + 2].rearrange("p j m t -> p (j m t)").bitcast(F32)
+            nc.scalar.copy(dst.rearrange("p (j m u) -> p j m u", j=2, u=2), vb.rearrange("p j u m -> p j m u"))
 
         def quantise_v(j0, j1):
             nc.vector.quantize_mx(out=vcode[:, j0 * P:j1 * P].bitcast(FP8X4), scales=vscale[:, j0 * P:j1 * P],
@@ -188,11 +189,12 @@ def tile_attend_ttagreement_pl_kernel(tc, query, dquery, query2, dquery2, keys_w
         r = [tile([P, I], F32, name="r%d" % k) for k in range(QT)]
         rbar = [tile([P, I], F32, name="rbar%d" % k) for k in range(QT)]
         for k in range(QT):
-            nc.scalar.activation(rbar[k][:], gap[k][:], ACT.Sigmoid, bias=shift[:, 3 - k:4 - k], scale=1.0)
-            nc.scalar.activation(r[k][:], gap[k][:], ACT.Sigmoid, bias=shift[:, k:k + 1], scale=-1.0)
+            nc.scalar.activation(rbar[k][:], gap[k][:], ACT.Sigmoid, bias=shift[:, 3 - k:4 - k], scale=-1.0)
+            nc.scalar.activation(r[k][:], gap[k][:], ACT.Sigmoid, bias=shift[:, k:k + 1], scale=1.0)
 
-        values(0)
-        values(1)
+        gather_values(0)
+        gather_values(1)
+        turn_values(0)
         wgrp = tile([P, Q, PACK], BF16, name="wgrp")
         wcode = tile([P, Q], U32, name="wcode")
         wscale = tile([P, Q], U8, name="wscale")
@@ -202,8 +204,8 @@ def tile_attend_ttagreement_pl_kernel(tc, query, dquery, query2, dquery2, keys_w
             h = tile([P, I], F32, name="h%d" % k)
             a1 = tile([P, I], F32, name="a1_%d" % k)
             a2 = tile([P, I], F32, name="a2_%d" % k)
-            nc.gpsimd.tensor_tensor(h[:], rbar[k][:], wa[k][:], ALU.mult)
-            ht = bank(k, "ht%d" % k)
+            nc.vector.scalar_tensor_tensor(h[:], rbar[k][:], inv[:, k:k + 1], pa[k][:], ALU.mult, ALU.mult)
+            ht = bank(1 - k, "ht%d" % k)
             hs.append(tile([P, PACK, P], F32, name="hs%d" % k))
             for t in range(PACK):
                 nc.tensor.transpose(ht[:, t * P:(t + 1) * P], h[:, t * P:(t + 1) * P], ident[:])
@@ -212,14 +214,16 @@ def tile_attend_ttagreement_pl_kernel(tc, query, dquery, query2, dquery2, keys_w
             nc.vector.scalar_tensor_tensor(a1[:], ta[k][:], mean[:, k:k + 1], rbar[k][:], ALU.subtract, ALU.mult)
             nc.vector.scalar_tensor_tensor(a2[:], tb[k][:], mean[:, 3 - k:4 - k], r[k][:], ALU.subtract, ALU.mult)
             at.append(bank(4 + k, "at%d" % k))
-            for t in range(PACK):
-                cols = slice(t * P, (t + 1) * P)
-                nc.tensor.matmul(at[k][:, cols], a1[:, cols], ident[:], start=True, stop=False, is_transpose=True)
-                nc.tensor.matmul(at[k][:, cols], a2[:, cols], ident[:], start=False, stop=True, is_transpose=True)
+            for n, term in enumerate((a1, a2)):
+                for t in range(PACK):
+                    cols = slice(t * P, (t + 1) * P)
+                    nc.tensor.matmul(at[k][:, cols], term[:, cols], ident[:], start=(n == 0 and t == 0),
+                                     stop=(n == 1 and t == PACK - 1), is_transpose=True)
 
         def weigh(k):
-            nc.vector.tensor_tensor(wgrp[:, k * P:(k + 1) * P, :], at[k][:].rearrange("p (t q) -> p q t", t=PACK),
-                                    hs[k][:].rearrange("p t q -> p q t"), ALU.mult)
+            nc.vector.tensor_tensor(wgrp[:, k * P:(k + 1) * P, :].rearrange("p (c i) t -> p c t i", i=4),
+                                    at[k][:].rearrange("p (t c i) -> p c t i", t=PACK, i=4),
+                                    hs[k][:].rearrange("p t (c i) -> p c t i", i=4), ALU.mult)
 
         def quantise_w(k):
             cols = slice(k * P, (k + 1) * P)
@@ -242,7 +246,7 @@ def tile_attend_ttagreement_pl_kernel(tc, query, dquery, query2, dquery2, keys_w
             regroup_out = nc.scalar.copy if k == 0 else nc.vector.tensor_copy
             regroup_out(ogrp[:, cols, :], ob[:].rearrange("p (j q) -> p q j", j=PACK))
             nc.scalar.copy(osb[:, :, cols], ob[:].rearrange("p (j q) -> p j q", j=PACK))
-            nc.sync.dma_start(out_rows[:, :, cols], osb[:, :, cols])
+            (nc.sync if k == 0 else nc.scalar).dma_start(out_rows[:, :, cols], osb[:, :, cols])
 
         def quantise_out(k):
             cols = slice(k * P, (k + 1) * P)
@@ -250,12 +254,12 @@ def tile_attend_ttagreement_pl_kernel(tc, query, dquery, query2, dquery2, keys_w
                                   in_=ogrp[:, cols, :].rearrange("p q t -> p (q t)"))
 
         terms(0)
-        quantise_v(0, 2)
-        values(2)
-        values(3)
+        gather_values(2)
+        gather_values(3)
+        turn_values(1)
         terms(1)
         weigh(0)
-        quantise_v(2, 4)
+        quantise_v(0, 4)
         quantise_w(0)
         product(0)
         weigh(1)

@@ -41,7 +41,11 @@ def tile_attend_ttagreement_pl_kernel(tc, query, dquery, query2, dquery2, keys_w
         kscale = tile([P, T], U8, name="kscale")
         nc.gpsimd.memset(kscale[:].bitcast(I32), 0)
         kword = tile([P, T], U16, name="kword")
-        nc.sync.dma_start(kword[:].bitcast(I32), keys_words[0].bitcast(I32))
+        for half in range(2):
+            cols = slice(half * T // 4, (half + 1) * T // 4)
+            nc.sync.dma_start(kword[:].bitcast(I32)[:, cols], keys_words[0].bitcast(I32)[:, cols])
+        os_col = tile([P, PACK], F32, name="os_col")
+        nc.sync.dma_start(os_col[:], slot_factor.rearrange("o (s t) -> (o s) t", t=PACK))
         for g in range(4):
             nc.scalar.dma_start(kscale[32 * g:32 * g + 4, :].bitcast(I32),
                                 keys_scales[0, 4 * g:4 * g + 4, :].bitcast(I32))
@@ -50,16 +54,16 @@ def tile_attend_ttagreement_pl_kernel(tc, query, dquery, query2, dquery2, keys_w
         qraw = {}
 
         def load_query(n):
-            qraw[n] = tile([P, PACK, Q], F32, name="raw_" + n, slot="kword" if n == "db" else None)
+            qraw[n] = tile([P, PACK, Q], F32, name="raw_" + n)
             nc.sync.dma_start(qraw[n][:], qsrc[n].rearrange("(p j) q -> p j q", j=PACK))
 
-        for n in qnames[:3]:
+        for n in qnames:
             load_query(n)
         vraw = []
         vals_dealt = vals.rearrange("(p j) t -> j p t", j=PACK)
 
-        def load_values(j, slot):
-            vraw.append(tile([P, T], F32, name="vraw%d" % j, slot=slot))
+        for j in range(PACK):
+            vraw.append(tile([P, T], F32, name="vraw%d" % j))
             nc.sync.dma_start(vraw[j][:], vals_dealt[j])
 
         ident = tile([P, P], F32, name="ident")
@@ -74,10 +78,6 @@ def tile_attend_ttagreement_pl_kernel(tc, query, dquery, query2, dquery2, keys_w
         nc.vector.tensor_copy(kw_d[:].rearrange("p (t s) -> p t s", t=PACK), kw_g[:].rearrange("p (s t) -> p t s", t=PACK))
         nc.vector.tensor_copy(ks_d[:].rearrange("p (t s) -> p t s", t=PACK), ks_g[:].rearrange("p (s t) -> p t s", t=PACK))
 
-        load_query("db")
-        load_values(0, "ks_g")
-        os_col = tile([P, PACK], F32, name="os_col", slot="kw_g")
-        nc.sync.dma_start(os_col[:], slot_factor.rearrange("o (s t) -> (o s) t", t=PACK))
 
         qcode, qscale = {}, {}
 
@@ -105,19 +105,17 @@ def tile_attend_ttagreement_pl_kernel(tc, query, dquery, query2, dquery2, keys_w
         junk = [tile([P, I], F32, name="junk%d" % k) for k in range(2 * QT)]
 
         quantise_q("qa", regroup("qa"))
-        load_values(1, "raw_qa")
         sa = [bank(k, "sa%d" % k) for k in range(QT)]
         for k in range(QT):
             score(sa[k], "qa", k)
         quantise_q("qb", regroup("qb"))
-        load_values(2, "raw_qb")
         sb_neg = [bank(2 + k, "sbn%d" % k) for k in range(QT)]
         for k in range(QT):
             score(sb_neg[k], "qb", k)
         g_da = regroup("da")
-        load_values(3, "raw_da")
         g_db = regroup("db")
         nega = tile([P, I], F32, name="nega")
+        negb = tile([P, I], F32, name="negb")
         pa = [tile([P, I], F32, name="pa%d" % k) for k in range(QT)]
         pb = [tile([P, I], F32, name="pb%d" % k) for k in range(QT)]
         for k in range(QT):
@@ -127,35 +125,41 @@ def tile_attend_ttagreement_pl_kernel(tc, query, dquery, query2, dquery2, keys_w
                 nc.vector.tensor_reduce(negmax[:, k:k + 1], sa[k][:], AX.X, ALU.max, negate=True)
             nc.scalar.activation(pa[k][:], sa[k][:], ACT.Exp, bias=negmax[:, k:k + 1], scale=1.0,
                                  accum_out=rowsum[:, k:k + 1])
-        for k in range(QT):
-            nc.vector.tensor_reduce(negmax[:, 3 - k:4 - k], sb_neg[k][:], AX.X, ALU.min)
-            nc.scalar.activation(pb[k][:], sb_neg[k][:], ACT.Exp, bias=negmax[:, 3 - k:4 - k], scale=-1.0,
-                                 accum_out=rowsum[:, 3 - k:4 - k])
         quantise_q("da", g_da)
         ta = [bank(4 + k, "ta%d" % k) for k in range(QT)]
         for k in range(QT):
             score(ta[k], "da", k)
+        for k in range(QT):
+            if k == 0:
+                nc.vector.tensor_scalar(negb[:], sb_neg[k][:], 1.0, None, ALU.mult, ALU.min, accum_out=negmax[:, 3:4])
+            else:
+                nc.vector.tensor_reduce(negmax[:, 3 - k:4 - k], sb_neg[k][:], AX.X, ALU.min)
+            nc.scalar.activation(pb[k][:], sb_neg[k][:], ACT.Exp, bias=negmax[:, 3 - k:4 - k], scale=-1.0,
+                                 accum_out=rowsum[:, 3 - k:4 - k])
         quantise_q("db", g_db)
         tb = [bank(6 + k, "tb%d" % k) for k in range(QT)]
         for k in range(QT):
             score(tb[k], "db", k)
-        gap = [tile([P, I], F32, name="gap0"), bank(0, "gap1")]
-        nc.vector.tensor_tensor(gap[0][:], sb_neg[0][:], nega[:], ALU.subtract)
+        gap = [tile([P, I], F32, name="gap0", slot="grp_db"), bank(0, "gap1")]
+        nc.gpsimd.tensor_tensor(gap[0][:], negb[:], nega[:], ALU.subtract)
         score(gap[1], "qa", 1, stop=False)
         score(gap[1], "qb", 1, start=False)
-        logsum = tile([P, 4], F32, name="logsum")
-        nc.scalar.activation(logsum[:], rowsum[:], ACT.Ln)
-
-
+        inv = tile([P, 4], F32, name="inv")
+        nc.vector.reciprocal(inv[:], rowsum[:])
+        ratio = tile([P, 4], F32, name="ratio")
+        nc.vector.tensor_tensor(ratio[:], rowsum[:, ::-1], inv[:], ALU.mult)
+        maxgap = tile([P, 4], F32, name="maxgap")
+        nc.vector.tensor_tensor(maxgap[:], negmax[:, ::-1], negmax[:], ALU.subtract)
+        logratio = tile([P, 4], F32, name="logratio")
+        nc.scalar.activation(logratio[:], ratio[:], ACT.Ln)
+        shift = tile([P, 4], F32, name="shift")
+        nc.vector.tensor_tensor(shift[:], logratio[:], maxgap[:], ALU.subtract)
         for k in range(QT):
             nc.vector.scalar_tensor_tensor(junk[k][:], ta[k][:], 1.0, pa[k][:], ALU.mult, ALU.mult,
                                            accum_out=tsum[:, k:k + 1])
-        inv = tile([P, 4], F32, name="inv")
-        nc.vector.reciprocal(inv[:], rowsum[:])
-        lse = tile([P, 4], F32, name="lse")
-        nc.vector.tensor_tensor(lse[:], logsum[:], negmax[:], ALU.subtract)
-        shift = tile([P, 4], F32, name="shift")
-        nc.vector.tensor_tensor(shift[:], lse[:, ::-1], lse[:], ALU.subtract)
+        wa = [tile([P, I], F32, name="wa%d" % k) for k in range(QT)]
+        for k in range(QT):
+            nc.gpsimd.tensor_scalar(wa[k][:], pa[k][:], inv[:, k:k + 1], 0.0, ALU.mult, ALU.add)
         for k in range(QT):
             nc.vector.scalar_tensor_tensor(junk[2 + k][:], tb[k][:], 1.0, pb[k][:], ALU.mult, ALU.mult,
                                            accum_out=tsum[:, 3 - k:4 - k])
@@ -163,14 +167,12 @@ def tile_attend_ttagreement_pl_kernel(tc, query, dquery, query2, dquery2, keys_w
         nc.vector.tensor_tensor(mean[:], tsum[:], inv[:], ALU.mult)
 
         vgrp = tile([P, PACK, P, PACK], BF16, name="vgrp", slot="shift")
-        vcode = tile([P, E], U32, name="vcode")
+        vcode = tile([P, E], U32, name="vcode", slot="vraw2")
         vscale = tile([P, E], U8, name="vscale")
-        vg, vpair = {}, {}
+        vg = {}
 
         def gather_values(j):
-            if j % 2 == 0:
-                vpair[j // 2] = tile([P, 2, I], BF16, name="vg%d" % j, slot=("lse", "r0")[j // 2])
-            vg[j] = vpair[j // 2][:, j % 2, :]
+            vg[j] = tile([P, I], BF16, name="vg%d" % j, slot=("pb0", "ratio", "r0", "rbar0")[j])[:]
             nc.vector.tensor_copy(vg[j], vraw[j][:].indirect(offsets[:]))
 
         def turn_values(pair):
@@ -196,15 +198,15 @@ def tile_attend_ttagreement_pl_kernel(tc, query, dquery, query2, dquery2, keys_w
         gather_values(1)
         turn_values(0)
         wgrp = tile([P, Q, PACK], BF16, name="wgrp")
-        wcode = tile([P, Q], U32, name="wcode")
+        wcode = tile([P, Q], U32, name="wcode", slot="hs1")
         wscale = tile([P, Q], U8, name="wscale")
         hs, at = [], []
 
         def terms(k):
-            h = tile([P, I], F32, name="h%d" % k)
+            h = tile([P, I], F32, name="h%d" % k, slot=("vraw1", "vraw0")[k])
             a1 = tile([P, I], F32, name="a1_%d" % k)
             a2 = tile([P, I], F32, name="a2_%d" % k)
-            nc.vector.scalar_tensor_tensor(h[:], rbar[k][:], inv[:, k:k + 1], pa[k][:], ALU.mult, ALU.mult)
+            nc.gpsimd.tensor_tensor(h[:], rbar[k][:], wa[k][:], ALU.mult)
             ht = bank(1 - k, "ht%d" % k)
             hs.append(tile([P, PACK, P], F32, name="hs%d" % k))
             for t in range(PACK):
@@ -236,37 +238,42 @@ def tile_attend_ttagreement_pl_kernel(tc, query, dquery, query2, dquery2, keys_w
         oscale = tile([P, Q], U8, name="oscale")
         out_rows = out_0.rearrange("(p j) q -> p j q", j=PACK)
 
-        def product(k):
+        def product(k, j):
             cols = slice(k * P, (k + 1) * P)
-            ob = bank(6 + k, "ob%d" % k)
-            for j in range(PACK):
-                ecols = slice(j * P, (j + 1) * P)
-                nc.tensor.matmul_mx(out=ob[:, ecols], lhsT=vcode[:, ecols].bitcast(FP8X4), lhsT_scale=vscale[:, ecols],
-                                    rhs=wcode[:, cols].bitcast(FP8X4), rhs_scale=wscale[:, cols], start=True, stop=True)
-            regroup_out = nc.scalar.copy if k == 0 else nc.vector.tensor_copy
-            regroup_out(ogrp[:, cols, :], ob[:].rearrange("p (j q) -> p q j", j=PACK))
-            nc.scalar.copy(osb[:, :, cols], ob[:].rearrange("p (j q) -> p j q", j=PACK))
+            ecols = slice(j * P, (j + 1) * P)
+            nc.tensor.matmul_mx(out=obs[k][:, ecols], lhsT=vcode[:, ecols].bitcast(FP8X4), lhsT_scale=vscale[:, ecols],
+                                rhs=wcode[:, cols].bitcast(FP8X4), rhs_scale=wscale[:, cols], start=True, stop=True)
+
+        def regroup_out(k):
+            move = nc.scalar.copy if k == 0 else nc.vector.tensor_copy
+            move(ogrp[:, k * P:(k + 1) * P, :], obs[k][:].rearrange("p (j q) -> p q j", j=PACK))
+
+        def copy_out(k):
+            cols = slice(k * P, (k + 1) * P)
+            nc.scalar.copy(osb[:, :, cols], obs[k][:].rearrange("p (j q) -> p j q", j=PACK))
             (nc.sync if k == 0 else nc.scalar).dma_start(out_rows[:, :, cols], osb[:, :, cols])
 
-        def quantise_out(k):
-            cols = slice(k * P, (k + 1) * P)
-            nc.vector.quantize_mx(out=ocode[:, cols].bitcast(FP8X4), scales=oscale[:, cols],
-                                  in_=ogrp[:, cols, :].rearrange("p q t -> p (q t)"))
-
         terms(0)
+        terms(1)
         gather_values(2)
         gather_values(3)
         turn_values(1)
-        terms(1)
+        quantise_v(0, 2)
         weigh(0)
-        quantise_v(0, 4)
-        quantise_w(0)
-        product(0)
         weigh(1)
+        quantise_v(2, 4)
+        quantise_w(0)
         quantise_w(1)
-        quantise_out(0)
-        product(1)
-        quantise_out(1)
+        obs = [bank(6 + k, "ob%d" % k) for k in range(QT)]
+        for k in range(QT):
+            for j in range(PACK):
+                product(k, j)
+        regroup_out(0)
+        regroup_out(1)
+        copy_out(0)
+        copy_out(1)
+        nc.vector.quantize_mx(out=ocode[:].bitcast(FP8X4), scales=oscale[:],
+                              in_=ogrp[:].rearrange("p q t -> p (q t)"))
         nc.sync.dma_start(out_1[0].rearrange("p c r -> p (c r)").bitcast(I32), ocode[:].bitcast(I32))
         for g in range(4):
             queue = nc.scalar if g % 2 else nc.sync

@@ -41,14 +41,7 @@ def tile_attend_ttagreement_pl_kernel(tc, query, dquery, query2, dquery2, keys_w
         kscale = tile([P, T], U8, name="kscale")
         nc.gpsimd.memset(kscale[:].bitcast(I32), 0)
         kword = tile([P, T], U16, name="kword")
-        for half in range(2):
-            cols = slice(half * T // 4, (half + 1) * T // 4)
-            nc.sync.dma_start(kword[:].bitcast(I32)[:, cols], keys_words[0].bitcast(I32)[:, cols])
-        os_col = tile([P, PACK], F32, name="os_col")
-        nc.sync.dma_start(os_col[:], slot_factor.rearrange("o (s t) -> (o s) t", t=PACK))
-        for g in range(4):
-            nc.scalar.dma_start(kscale[32 * g:32 * g + 4, :].bitcast(I32),
-                                keys_scales[0, 4 * g:4 * g + 4, :].bitcast(I32))
+        nc.sync.dma_start(kword[:].bitcast(I32), keys_words[0].bitcast(I32))
         qnames = ("qa", "qb", "da", "db")
         qsrc = dict(zip(qnames, (query, query2, dquery, dquery2)))
         qraw = {}
@@ -57,7 +50,13 @@ def tile_attend_ttagreement_pl_kernel(tc, query, dquery, query2, dquery2, keys_w
             qraw[n] = tile([P, PACK, Q], F32, name="raw_" + n)
             nc.sync.dma_start(qraw[n][:], qsrc[n].rearrange("(p j) q -> p j q", j=PACK))
 
-        for n in qnames:
+        load_query("qa")
+        os_col = tile([P, PACK], F32, name="os_col")
+        nc.sync.dma_start(os_col[:], slot_factor.rearrange("o (s t) -> (o s) t", t=PACK))
+        for g in range(4):
+            nc.sync.dma_start(kscale[32 * g:32 * g + 4, :].bitcast(I32),
+                              keys_scales[0, 4 * g:4 * g + 4, :].bitcast(I32))
+        for n in qnames[1:]:
             load_query(n)
         vraw = []
         vals_dealt = vals.rearrange("(p j) t -> j p t", j=PACK)
@@ -99,7 +98,6 @@ def tile_attend_ttagreement_pl_kernel(tc, query, dquery, query2, dquery2, keys_w
             nc.tensor.matmul_mx(out=out[:], lhsT=qcode[n][:, cols].bitcast(FP8X4), lhsT_scale=qscale[n][:, cols],
                                 rhs=kw_d[:].bitcast(FP4X4), rhs_scale=ks_d[:], start=start, stop=stop)
 
-        negmax = tile([P, 4], F32, name="negmax")
         rowsum = tile([P, 4], F32, name="rowsum")
         tsum = tile([P, 4], F32, name="tsum")
         junk = [tile([P, I], F32, name="junk%d" % k) for k in range(2 * QT)]
@@ -109,6 +107,7 @@ def tile_attend_ttagreement_pl_kernel(tc, query, dquery, query2, dquery2, keys_w
         for k in range(QT):
             score(sa[k], "qa", k)
         quantise_q("qb", regroup("qb"))
+        negmax = tile([P, 4], F32, name="negmax", slot="grp_qb")
         sb_neg = [bank(2 + k, "sbn%d" % k) for k in range(QT)]
         for k in range(QT):
             score(sb_neg[k], "qb", k)
@@ -116,14 +115,15 @@ def tile_attend_ttagreement_pl_kernel(tc, query, dquery, query2, dquery2, keys_w
         g_db = regroup("db")
         nega = tile([P, I], F32, name="nega")
         negb = tile([P, I], F32, name="negb")
-        pa = [tile([P, I], F32, name="pa%d" % k) for k in range(QT)]
+        pa_both = tile([P, QT, I], F32, name="pa", slot="raw_db")
+        pa = [pa_both[:, k, :] for k in range(QT)]
         pb = [tile([P, I], F32, name="pb%d" % k) for k in range(QT)]
         for k in range(QT):
             if k == 0:
                 nc.vector.tensor_scalar(nega[:], sa[k][:], -1.0, None, ALU.mult, ALU.min, accum_out=negmax[:, k:k + 1])
             else:
                 nc.vector.tensor_reduce(negmax[:, k:k + 1], sa[k][:], AX.X, ALU.max, negate=True)
-            nc.scalar.activation(pa[k][:], sa[k][:], ACT.Exp, bias=negmax[:, k:k + 1], scale=1.0,
+            nc.scalar.activation(pa[k], sa[k][:], ACT.Exp, bias=negmax[:, k:k + 1], scale=1.0,
                                  accum_out=rowsum[:, k:k + 1])
         quantise_q("da", g_da)
         ta = [bank(4 + k, "ta%d" % k) for k in range(QT)]
@@ -140,26 +140,25 @@ def tile_attend_ttagreement_pl_kernel(tc, query, dquery, query2, dquery2, keys_w
         tb = [bank(6 + k, "tb%d" % k) for k in range(QT)]
         for k in range(QT):
             score(tb[k], "db", k)
-        gap = [tile([P, I], F32, name="gap0", slot="grp_db"), bank(0, "gap1")]
+        gap = [tile([P, I], F32, name="gap0", slot="grp_db"), bank(3, "gap1")]
         nc.gpsimd.tensor_tensor(gap[0][:], negb[:], nega[:], ALU.subtract)
         score(gap[1], "qa", 1, stop=False)
         score(gap[1], "qb", 1, start=False)
         inv = tile([P, 4], F32, name="inv")
         nc.vector.reciprocal(inv[:], rowsum[:])
-        ratio = tile([P, 4], F32, name="ratio")
-        nc.vector.tensor_tensor(ratio[:], rowsum[:, ::-1], inv[:], ALU.mult)
         maxgap = tile([P, 4], F32, name="maxgap")
         nc.vector.tensor_tensor(maxgap[:], negmax[:, ::-1], negmax[:], ALU.subtract)
         logratio = tile([P, 4], F32, name="logratio")
-        nc.scalar.activation(logratio[:], ratio[:], ACT.Ln)
+        for c in range(4):
+            nc.scalar.activation(logratio[:, c:c + 1], rowsum[:, 3 - c:4 - c], ACT.Ln, scale=inv[:, c:c + 1])
         shift = tile([P, 4], F32, name="shift")
         nc.vector.tensor_tensor(shift[:], logratio[:], maxgap[:], ALU.subtract)
         for k in range(QT):
-            nc.vector.scalar_tensor_tensor(junk[k][:], ta[k][:], 1.0, pa[k][:], ALU.mult, ALU.mult,
+            nc.vector.scalar_tensor_tensor(junk[k][:], ta[k][:], 1.0, pa[k], ALU.mult, ALU.mult,
                                            accum_out=tsum[:, k:k + 1])
         wa = [tile([P, I], F32, name="wa%d" % k) for k in range(QT)]
         for k in range(QT):
-            nc.gpsimd.tensor_scalar(wa[k][:], pa[k][:], inv[:, k:k + 1], 0.0, ALU.mult, ALU.add)
+            nc.gpsimd.tensor_scalar(wa[k][:], pa[k], inv[:, k:k + 1], 0.0, ALU.mult, ALU.add)
         for k in range(QT):
             nc.vector.scalar_tensor_tensor(junk[2 + k][:], tb[k][:], 1.0, pb[k][:], ALU.mult, ALU.mult,
                                            accum_out=tsum[:, 3 - k:4 - k])
@@ -172,17 +171,17 @@ def tile_attend_ttagreement_pl_kernel(tc, query, dquery, query2, dquery2, keys_w
         vg = {}
 
         def gather_values(j):
-            vg[j] = tile([P, I], BF16, name="vg%d" % j, slot=("pb0", "ratio", "r0", "rbar0")[j])[:]
+            vg[j] = tile([P, I], BF16, name="vg%d" % j, slot=("pb0", "rowsum", "r0", "rbar0")[j])[:]
             nc.vector.tensor_copy(vg[j], vraw[j][:].indirect(offsets[:]))
 
-        def turn_values(pair):
-            vb = bank(2 + pair, "vbank%d" % pair)[:].rearrange("p (j u m) -> p j u m", j=2, u=2)
-            for j in range(2):
-                words = vg[2 * pair + j].bitcast(F32)
+        def turn_values(j0, count, bank_no):
+            vb = bank(bank_no, "vbank%d" % j0)[:, :count * I // 2].rearrange("p (j u m) -> p j u m", j=count, u=2)
+            for j in range(count):
+                words = vg[j0 + j].bitcast(F32)
                 for u in range(2):
                     nc.tensor.transpose(vb[:, j, u, :], words[:, u:I // 2:2], ident[:])
-            dst = vgrp[:, 2 * pair:2 * pair + 2].rearrange("p j m t -> p (j m t)").bitcast(F32)
-            nc.scalar.copy(dst.rearrange("p (j m u) -> p j m u", j=2, u=2), vb.rearrange("p j u m -> p j m u"))
+            dst = vgrp[:, j0:j0 + count].rearrange("p j m t -> p (j m t)").bitcast(F32)
+            nc.scalar.copy(dst.rearrange("p (j m u) -> p j m u", j=count, u=2), vb.rearrange("p j u m -> p j m u"))
 
         def quantise_v(j0, j1):
             nc.vector.quantize_mx(out=vcode[:, j0 * P:j1 * P].bitcast(FP8X4), scales=vscale[:, j0 * P:j1 * P],
@@ -196,7 +195,7 @@ def tile_attend_ttagreement_pl_kernel(tc, query, dquery, query2, dquery2, keys_w
 
         gather_values(0)
         gather_values(1)
-        turn_values(0)
+        turn_values(0, 2, 0)
         wgrp = tile([P, Q, PACK], BF16, name="wgrp")
         wcode = tile([P, Q], U32, name="wcode", slot="hs1")
         wscale = tile([P, Q], U8, name="wscale")
@@ -207,7 +206,7 @@ def tile_attend_ttagreement_pl_kernel(tc, query, dquery, query2, dquery2, keys_w
             a1 = tile([P, I], F32, name="a1_%d" % k)
             a2 = tile([P, I], F32, name="a2_%d" % k)
             nc.gpsimd.tensor_tensor(h[:], rbar[k][:], wa[k][:], ALU.mult)
-            ht = bank(1 - k, "ht%d" % k)
+            ht = bank((1, 3)[k], "ht%d" % k)
             hs.append(tile([P, PACK, P], F32, name="hs%d" % k))
             for t in range(PACK):
                 nc.tensor.transpose(ht[:, t * P:(t + 1) * P], h[:, t * P:(t + 1) * P], ident[:])
@@ -256,12 +255,14 @@ def tile_attend_ttagreement_pl_kernel(tc, query, dquery, query2, dquery2, keys_w
         terms(0)
         terms(1)
         gather_values(2)
+        turn_values(2, 1, 2)
         gather_values(3)
-        turn_values(1)
+        turn_values(3, 1, 0)
         quantise_v(0, 2)
         weigh(0)
+        quantise_v(2, 3)
         weigh(1)
-        quantise_v(2, 4)
+        quantise_v(3, 4)
         quantise_w(0)
         quantise_w(1)
         obs = [bank(6 + k, "ob%d" % k) for k in range(QT)]

from contextlib import ExitStack

import concourse.mybir as mybir
from concourse.masks import make_identity

D, E, T, I, Q = 512, 512, 2048, 512, 256
FLOPS = 2 * (4 * D * Q * I + I * E * Q)

F32 = mybir.dt.float32
BF16 = mybir.dt.bfloat16
I32 = mybir.dt.int32
U32 = mybir.dt.uint32
U16 = mybir.dt.uint16
U8 = mybir.dt.uint8
FP8X4 = mybir.dt.float8_e4m3fn_x4
FP4X4 = mybir.dt.float4_e2m1fn_x4
ALU = mybir.AluOpType
AX = mybir.AxisListType
ACT = mybir.ActivationFunctionType

P = 128
PACK = 4
QT = Q // P


def tile_attend_ttagreement_pl_kernel(tc, query, dquery, query2, dquery2, keys_words, keys_scales, slot_factor, vals, offs,
                                       out_0, out_1, out_2):
    nc = tc.nc
    with ExitStack() as ctx:
        sb = ctx.enter_context(tc.tile_pool(name="sb", bufs=1))
        ps = ctx.enter_context(tc.psum_pool(name="ps", bufs=1))

        def tile(shape, dtype, name, slot=None):
            return sb.tile(shape, dtype, name=name, tag=slot or name, align_bytes=64)

        def bank(n, name):
            return ps.tile([P, 512], F32, name=name, tag="bank%d" % n)

        offsets = tile([P, I // 16], U16, name="offsets")
        nc.sync.dma_start(offsets[:], offs)
        kscale = tile([P, T], U8, name="kscale")
        nc.gpsimd.memset(kscale[:].bitcast(I32), 0)
        kword = tile([P, T], U16, name="kword")
        nc.sync.dma_start(kword[:].bitcast(I32), keys_words[0].bitcast(I32))
        qnames = ("qa", "qb", "da", "db")
        qsrc = dict(zip(qnames, (query, query2, dquery, dquery2)))
        qraw = {}

        def load_query(n):
            qraw[n] = tile([P, PACK, Q], F32, name="raw_" + n)
            nc.sync.dma_start(qraw[n][:], qsrc[n].rearrange("(p j) q -> p j q", j=PACK))

        load_query("qa")
        os_col = tile([P, PACK], F32, name="os_col")
        nc.sync.dma_start(os_col[:], slot_factor.rearrange("o (s t) -> (o s) t", t=PACK))
        for g in range(4):
            nc.sync.dma_start(kscale[32 * g:32 * g + 4, :].bitcast(I32),
                              keys_scales[0, 4 * g:4 * g + 4, :].bitcast(I32))
        for n in qnames[1:]:
            load_query(n)
        vraw = []
        vals_dealt = vals.rearrange("(p j) t -> j p t", j=PACK)

        for j in range(PACK):
            vraw.append(tile([P, T], F32, name="vraw%d" % j))
            nc.sync.dma_start(vraw[j][:], vals_dealt[j])

        ident = tile([P, P], F32, name="ident")
        make_identity(nc, ident[:])

        ks_g = tile([P, I], U8, name="ks_g")
        kw_g = tile([P, I], U16, name="kw_g")
        ks_d = tile([P, I], U8, name="ks_d")
        kw_d = tile([P, I], U16, name="kw_d")
        nc.vector.tensor_copy(kw_g[:], kword[:].indirect(offsets[:]))
        nc.vector.tensor_copy(ks_g[:], kscale[:].indirect(offsets[:]))
        nc.vector.tensor_copy(kw_d[:].rearrange("p (t s) -> p t s", t=PACK), kw_g[:].rearrange("p (s t) -> p t s", t=PACK))
        nc.vector.tensor_copy(ks_d[:].rearrange("p (t s) -> p t s", t=PACK), ks_g[:].rearrange("p (s t) -> p t s", t=PACK))


        qcode, qscale = {}, {}

        def regroup(n):
            grouped = tile([P, Q, PACK], BF16, name="grp_" + n)
            dst = grouped[:].rearrange("p (c i) t -> p c t i", i=4)
            src = qraw[n][:].rearrange("p t (c i) -> p c t i", i=4)
            nc.scalar.activation(dst, src, ACT.Copy, scale=-1.0 if n == "qb" else 1.0)
            return grouped

        def quantise_q(n, grouped):
            qcode[n] = tile([P, Q], U32, name="code_" + n, slot="kscale" if n == "qa" else None)
            qscale[n] = tile([P, Q], U8, name="scale_" + n)
            nc.vector.quantize_mx(out=qcode[n][:].bitcast(FP8X4), scales=qscale[n][:],
                                  in_=grouped[:].rearrange("p q t -> p (q t)"))

        def score(out, n, k, start=True, stop=True):
            cols = slice(k * P, (k + 1) * P)
            nc.tensor.matmul_mx(out=out[:], lhsT=qcode[n][:, cols].bitcast(FP8X4), lhsT_scale=qscale[n][:, cols],
                                rhs=kw_d[:].bitcast(FP4X4), rhs_scale=ks_d[:], start=start, stop=stop)

        rowsum = tile([P, 4], F32, name="rowsum")
        tsum = tile([P, 4], F32, name="tsum")
        junk = [tile([P, I], F32, name="junk%d" % k) for k in range(2 * QT)]

        quantise_q("qa", regroup("qa"))
        sa = [bank(k, "sa%d" % k) for k in range(QT)]
        for k in range(QT):
            score(sa[k], "qa", k)
        quantise_q("qb", regroup("qb"))
        negmax = tile([P, 4], F32, name="negmax", slot="grp_qb")
        sb_neg = [bank(2 + k, "sbn%d" % k) for k in range(QT)]
        for k in range(QT):
            score(sb_neg[k], "qb", k)
        g_da = regroup("da")
        g_db = regroup("db")
        nega = tile([P, I], F32, name="nega")
        negb = tile([P, I], F32, name="negb")
        pa_both = tile([P, QT, I], F32, name="pa", slot="raw_db")
        pa = [pa_both[:, k, :] for k in range(QT)]
        pb = [tile([P, I], F32, name="pb%d" % k) for k in range(QT)]
        for k in range(QT):
            if k == 0:
                nc.vector.tensor_scalar(nega[:], sa[k][:], -1.0, None, ALU.mult, ALU.min, accum_out=negmax[:, k:k + 1])
            else:
                nc.vector.tensor_reduce(negmax[:, k:k + 1], sa[k][:], AX.X, ALU.max, negate=True)
            nc.scalar.activation(pa[k], sa[k][:], ACT.Exp, bias=negmax[:, k:k + 1], scale=1.0,
                                 accum_out=rowsum[:, k:k + 1])
        quantise_q("da", g_da)
        ta = [bank(4 + k, "ta%d" % k) for k in range(QT)]
        for k in range(QT):
            score(ta[k], "da", k)
        for k in range(QT):
            if k == 0:
                nc.vector.tensor_scalar(negb[:], sb_neg[k][:], 1.0, None, ALU.mult, ALU.min, accum_out=negmax[:, 3:4])
            else:
                nc.vector.tensor_reduce(negmax[:, 3 - k:4 - k], sb_neg[k][:], AX.X, ALU.min)
            nc.scalar.activation(pb[k][:], sb_neg[k][:], ACT.Exp, bias=negmax[:, 3 - k:4 - k], scale=-1.0,
                                 accum_out=rowsum[:, 3 - k:4 - k])
        quantise_q("db", g_db)
        tb = [bank(6 + k, "tb%d" % k) for k in range(QT)]
        for k in range(QT):
            score(tb[k], "db", k)
        gap = [tile([P, I], F32, name="gap0", slot="grp_db"), bank(3, "gap1")]
        nc.gpsimd.tensor_tensor(gap[0][:], negb[:], nega[:], ALU.subtract)
        score(gap[1], "qa", 1, stop=False)
        score(gap[1], "qb", 1, start=False)
        inv = tile([P, 4], F32, name="inv")
        nc.vector.reciprocal(inv[:], rowsum[:])
        maxgap = tile([P, 4], F32, name="maxgap")
        nc.vector.tensor_tensor(maxgap[:], negmax[:, ::-1], negmax[:], ALU.subtract)
        logratio = tile([P, 4], F32, name="logratio")
        for c in range(4):
            nc.scalar.activation(logratio[:, c:c + 1], rowsum[:, 3 - c:4 - c], ACT.Ln, scale=inv[:, c:c + 1])
        shift = tile([P, 4], F32, name="shift")
        nc.vector.tensor_tensor(shift[:], logratio[:], maxgap[:], ALU.subtract)
        for k in range(QT):
            nc.vector.scalar_tensor_tensor(junk[k][:], ta[k][:], 1.0, pa[k], ALU.mult, ALU.mult,
                                           accum_out=tsum[:, k:k + 1])
        wa = [tile([P, I], F32, name="wa%d" % k) for k in range(QT)]
        for k in range(QT):
            nc.gpsimd.tensor_scalar(wa[k][:], pa[k], inv[:, k:k + 1], 0.0, ALU.mult, ALU.add)
        for k in range(QT):
            nc.vector.scalar_tensor_tensor(junk[2 + k][:], tb[k][:], 1.0, pb[k][:], ALU.mult, ALU.mult,
                                           accum_out=tsum[:, 3 - k:4 - k])
        mean = tile([P, 4], F32, name="mean")
        nc.vector.tensor_tensor(mean[:], tsum[:], inv[:], ALU.mult)

        vgrp = tile([P, PACK, P, PACK], BF16, name="vgrp", slot="shift")
        vcode = tile([P, E], U32, name="vcode", slot="vraw2")
        vscale = tile([P, E], U8, name="vscale")
        vg = {}

        def gather_values(j):
            vg[j] = tile([P, I], BF16, name="vg%d" % j, slot=("pb0", "rowsum", "r0", "rbar0")[j])[:]
            nc.vector.tensor_copy(vg[j], vraw[j][:].indirect(offsets[:]))

        def turn_values(j0, count, bank_no):
            vb = bank(bank_no, "vbank%d" % j0)[:, :count * I // 2].rearrange("p (j u m) -> p j u m", j=count, u=2)
            for j in range(count):
                words = vg[j0 + j].bitcast(F32)
                for u in range(2):
                    nc.tensor.transpose(vb[:, j, u, :], words[:, u:I // 2:2], ident[:])
            dst = vgrp[:, j0:j0 + count].rearrange("p j m t -> p (j m t)").bitcast(F32)
            nc.scalar.copy(dst.rearrange("p (j m u) -> p j m u", j=count, u=2), vb.rearrange("p j u m -> p j m u"))

        def quantise_v(j0, j1):
            nc.vector.quantize_mx(out=vcode[:, j0 * P:j1 * P].bitcast(FP8X4), scales=vscale[:, j0 * P:j1 * P],
                                  in_=vgrp[:, j0:j1].rearrange("p j m t -> p (j m t)"))

        r = [tile([P, I], F32, name="r%d" % k) for k in range(QT)]
        rbar = [tile([P, I], F32, name="rbar%d" % k) for k in range(QT)]
        for k in range(QT):
            nc.scalar.activation(rbar[k][:], gap[k][:], ACT.Sigmoid, bias=shift[:, 3 - k:4 - k], scale=-1.0)
            nc.scalar.activation(r[k][:], gap[k][:], ACT.Sigmoid, bias=shift[:, k:k + 1], scale=1.0)

        gather_values(0)
        gather_values(1)
        turn_values(0, 2, 0)
        wgrp = tile([P, Q, PACK], BF16, name="wgrp")
        wcode = tile([P, Q], U32, name="wcode", slot="hs1")
        wscale = tile([P, Q], U8, name="wscale")
        hs, at = [], []

        def terms(k):
            h = tile([P, I], F32, name="h%d" % k, slot=("vraw1", "vraw0")[k])
            a1 = tile([P, I], F32, name="a1_%d" % k)
            a2 = tile([P, I], F32, name="a2_%d" % k)
            nc.gpsimd.tensor_tensor(h[:], rbar[k][:], wa[k][:], ALU.mult)
            ht = bank((1, 3)[k], "ht%d" % k)
            hs.append(tile([P, PACK, P], F32, name="hs%d" % k))
            for t in range(PACK):
                nc.tensor.transpose(ht[:, t * P:(t + 1) * P], h[:, t * P:(t + 1) * P], ident[:])
            for t in range(PACK):
                nc.scalar.activation(hs[k][:, t, :], ht[:, t * P:(t + 1) * P], ACT.Copy, scale=os_col[:, t:t + 1])
            nc.vector.scalar_tensor_tensor(a1[:], ta[k][:], mean[:, k:k + 1], rbar[k][:], ALU.subtract, ALU.mult)
            nc.vector.scalar_tensor_tensor(a2[:], tb[k][:], mean[:, 3 - k:4 - k], r[k][:], ALU.subtract, ALU.mult)
            at.append(bank(4 + k, "at%d" % k))
            for n, term in enumerate((a1, a2)):
                for t in range(PACK):
                    cols = slice(t * P, (t + 1) * P)
                    nc.tensor.matmul(at[k][:, cols], term[:, cols], ident[:], start=(n == 0 and t == 0),
                                     stop=(n == 1 and t == PACK - 1), is_transpose=True)

        def weigh(k):
            nc.vector.tensor_tensor(wgrp[:, k * P:(k + 1) * P, :].rearrange("p (c i) t -> p c t i", i=4),
                                    at[k][:].rearrange("p (t c i) -> p c t i", t=PACK, i=4),
                                    hs[k][:].rearrange("p t (c i) -> p c t i", i=4), ALU.mult)

        def quantise_w(k):
            cols = slice(k * P, (k + 1) * P)
            nc.vector.quantize_mx(out=wcode[:, cols].bitcast(FP8X4), scales=wscale[:, cols],
                                  in_=wgrp[:, cols, :].rearrange("p q t -> p (q t)"))

        osb = tile([P, PACK, Q], F32, name="osb")
        ogrp = tile([P, Q, PACK], BF16, name="ogrp")
        ocode = tile([P, Q], U32, name="ocode")
        oscale = tile([P, Q], U8, name="oscale")
        out_rows = out_0.rearrange("(p j) q -> p j q", j=PACK)

        def product(k, j):
            cols = slice(k * P, (k + 1) * P)
            ecols = slice(j * P, (j + 1) * P)
            nc.tensor.matmul_mx(out=obs[k][:, ecols], lhsT=vcode[:, ecols].bitcast(FP8X4), lhsT_scale=vscale[:, ecols],
                                rhs=wcode[:, cols].bitcast(FP8X4), rhs_scale=wscale[:, cols], start=True, stop=True)

        def regroup_out(k):
            move = nc.scalar.copy if k == 0 else nc.vector.tensor_copy
            move(ogrp[:, k * P:(k + 1) * P, :], obs[k][:].rearrange("p (j q) -> p q j", j=PACK))

        def copy_out(k):
            cols = slice(k * P, (k + 1) * P)
            nc.scalar.copy(osb[:, :, cols], obs[k][:].rearrange("p (j q) -> p j q", j=PACK))
            (nc.sync if k == 0 else nc.scalar).dma_start(out_rows[:, :, cols], osb[:, :, cols])

        terms(0)
        terms(1)
        gather_values(2)
        turn_values(2, 1, 2)
        gather_values(3)
        turn_values(3, 1, 0)
        quantise_v(0, 2)
        weigh(0)
        quantise_v(2, 3)
        weigh(1)
        quantise_v(3, 4)
        quantise_w(0)
        quantise_w(1)
        obs = [bank(6 + k, "ob%d" % k) for k in range(QT)]
        for k in range(QT):
            for j in range(PACK):
                product(k, j)
        regroup_out(0)
        regroup_out(1)
        copy_out(0)
        copy_out(1)
        nc.vector.quantize_mx(out=ocode[:].bitcast(FP8X4), scales=oscale[:],
                              in_=ogrp[:].rearrange("p q t -> p (q t)"))
        nc.sync.dma_start(out_1[0].rearrange("p c r -> p (c r)").bitcast(I32), ocode[:].bitcast(I32))
        for g in range(4):
            queue = nc.scalar if g % 2 else nc.sync
            queue.dma_start(out_2[0, 4 * g:4 * g + 4, :].bitcast(I32), oscale[32 * g:32 * g + 4, :].bitcast(I32))
